import numpy as np
import ml_dtypes


def mxq(x, axis, fmt="e4m3"):
    dtype, down = {"e4m3": (ml_dtypes.float8_e4m3fn, 7), "e5m2": (ml_dtypes.float8_e5m2, 14)}[fmt]
    v = np.moveaxis(np.asarray(x, np.float32).astype(ml_dtypes.bfloat16).astype(np.float64), axis, -1)
    blocks = v.reshape(v.shape[:-1] + (-1, 32))
    amax = np.abs(blocks).max(-1, keepdims=True)
    byte = np.maximum(np.where(amax > 0, np.frexp(amax)[1] - 1 + 127, 0) - down, 1)
    scale = np.exp2(byte - 127.0)
    codes = (blocks / scale).astype(np.float32).astype(dtype).astype(np.float64)
    return np.moveaxis((codes * scale).reshape(v.shape), -1, axis)


WIDE = False


def mx_kscale(k):
    if not WIDE:
        return np.ones(k)
    levels = np.array([10, -10, 5, -5, 0])
    if k % 512:
        return np.exp2(np.random.permutation(np.resize(levels, k // 32))).repeat(32)
    a = np.empty((k // 512, 16))
    for p in range(k // 512):
        a[p, :8] = np.random.permutation(np.resize(levels, 8))
        for g in range(8):
            far = levels[np.abs(levels - a[p, g]) >= 10]
            a[p, g + 8] = far[np.random.randint(len(far))]
    return np.exp2(a.ravel()).repeat(32)


def f64(x):
    return np.asarray(x).astype(np.float64)


def striped8(idx):
    return np.concatenate([x.reshape(-1, 16).T for x in idx]).astype(np.uint16)


def runs(offs, k):
    lists = np.stack([offs[16 * r : 16 * r + 16].T.reshape(-1) for r in range(8)]).astype(np.int64)
    return lists[np.arange(k) % 512 // 64]


def pack_weight(w):
    k, n = w.shape
    w = f64(np.asarray(w, np.float32).astype(ml_dtypes.bfloat16)).reshape(k // 32, 32, n)
    amax = np.abs(w).max(1)
    byte = np.clip(np.where(amax > 0, np.frexp(amax)[1] - 1 + 127 - 7, 1), 1, 254)
    scaled = (w * np.exp2(127.0 - byte)[:, None, :]).reshape(k, n).astype(np.float32)
    words = np.ascontiguousarray(scaled.reshape(k // 512, 128, 4, n).transpose(0, 1, 3, 2)).astype(ml_dtypes.float8_e4m3fn).view(np.uint8)
    return words, np.ascontiguousarray(byte.astype(np.uint8).reshape(k // 512, 16, n))


def unpack_weight(words, scales):
    g, p, n, _ = words.shape
    vals = np.ascontiguousarray(words).view(ml_dtypes.float8_e4m3fn).astype(np.float64) * np.repeat(np.exp2(scales.astype(np.float64) - 127.0), 8, axis=1)[..., None]
    return vals.transpose(0, 1, 3, 2).reshape(g * 512, n)


def sigmoid(v):
    return 1.0 / (1.0 + np.exp(-np.maximum(v, -700.0)))

def planes(y):
    n, m = y.shape
    v = y.astype(np.float32).astype(ml_dtypes.bfloat16).astype(np.float64).reshape(n // 32, 32, m)
    top = np.abs(v).max(1)
    byte = np.clip(np.where(top > 0, np.frexp(top)[1] - 1 + 127 - 7, 1), 1, 254)
    codes = (v * np.exp2(127.0 - byte)[:, None, :]).reshape(n, m).astype(np.float32).astype(ml_dtypes.float8_e4m3fn).view(np.uint8)
    words = codes.reshape(n // 512, 128, 4, m).transpose(0, 1, 3, 2)
    return np.ascontiguousarray(words), np.ascontiguousarray(byte.astype(np.uint8).reshape(n // 512, 16, m))


K, T, S, H, C = 512, 2048, 512, 512, 512


def setup_inputs():
    n = np.random.standard_normal
    s = mx_kscale(K)[:, None]
    packed_xT = pack_weight(n((K, T)) * s)
    packed_w1 = pack_weight(n((K, H)) / np.sqrt(K) / s)
    return {
        "x_words": packed_xT[0],
        "x_scales": packed_xT[1],
        "w1_words": packed_w1[0],
        "w1_scales": packed_w1[1],
        "gs": (np.random.uniform(0.5, 1.5, (K, 1)) / s).astype(np.float32),
        "offs": striped8(np.random.randint(0, T, (8, S))),
        "n1": striped8(np.stack([np.random.permutation(S) for _ in range(8)])),
        "n2": striped8(np.stack([np.random.permutation(S) for _ in range(8)])),
        "cand": striped8(np.random.randint(0, T, (8, C))),
        "n3": striped8(np.stack([np.random.permutation(S) for _ in range(8)])),
        "n4": striped8(np.stack([np.random.permutation(S) for _ in range(8)])),
    }


def reference(x_words, x_scales, w1_words, w1_scales, gs, offs, n1, n2, cand, n3, n4):
    x_cand = unpack_weight(x_words, x_scales)[np.arange(K)[:, None], runs(cand, K)]
    xq = unpack_weight(x_words, x_scales)[np.arange(K)[:, None], runs(offs, K)]
    y = unpack_weight(w1_words, w1_scales).T @ xq
    pa = y[np.arange(H)[:, None], runs(n1, H)]
    pb = y[np.arange(H)[:, None], runs(n2, H)]
    z = f64(gs) * (np.maximum(np.maximum(y, pa), pb) - (0.5 * (np.minimum(np.minimum(y, pa), pb))))
    s = 0.0625 * ((x_cand.T @ mxq(z, 0, "e4m3")))
    st = s[np.arange(C)[:, None], runs(n3, C)] - s
    out_0 = s * (sigmoid(st[np.arange(C)[:, None], runs(n4, C)]))
    return (out_0,) + planes(out_0)

@@ -1,0 +1,171 @@
+from contextlib import ExitStack
+
+import concourse.mybir as mybir
+
+K, T, S, H, C = 512, 2048, 512, 512, 512
+FLOPS = 2 * K * H * S + 2 * K * C * S
+
+F32 = mybir.dt.float32
+BF16 = mybir.dt.bfloat16
+I32 = mybir.dt.int32
+U32 = mybir.dt.uint32
+U16 = mybir.dt.uint16
+U8 = mybir.dt.uint8
+FP8X4 = mybir.dt.float8_e4m3fn_x4
+ALU = mybir.AluOpType
+ACT = mybir.ActivationFunctionType
+
+P = 128
+PACK = 4
+Z_CHUNKS = ((0, 256), (256, 128), (384, 128))
+HALVES = ((0, 256), (256, 256))
+
+
+def entries(offsets, start, count):
+    return offsets[:, start // 16 : (start + count) // 16]
+
+
+def tile_picked_hcandrangehopd_none_po_kernel(tc, x_words, x_scales, w1_words, w1_scales, gs, offs, n1, n2, cand, n3, n4, out_0, out_1, out_2):
+    nc = tc.nc
+    with ExitStack() as ctx:
+        lists = ctx.enter_context(tc.tile_pool(name="lists", bufs=1))
+        keep = ctx.enter_context(tc.tile_pool(name="keep", bufs=1))
+        psum = ctx.enter_context(tc.psum_pool(name="psum", bufs=1))
+
+        def load_list(name, src):
+            held = lists.tile([P, S // 16], U16, name=name)
+            nc.sync.dma_start(held[:], src)
+            return held
+
+        def zeroed_bytes(name, width):
+            held = keep.tile([P, width], U8, name=name, align_bytes=64)
+            nc.vector.memset(held[:].bitcast(I32), 0)
+            return held
+
+        table_scales = zeroed_bytes("table_scales", T)
+        w_scales_raw = zeroed_bytes("w_scales_raw", H)
+        xq_scales = zeroed_bytes("xq_scales", S)
+        cand_scales = zeroed_bytes("cand_scales", C)
+        offs_t = load_list("offs_t", offs)
+        cand_t = load_list("cand_t", cand)
+        n1_t = load_list("n1_t", n1)
+        n2_t = load_list("n2_t", n2)
+        table_words = keep.tile([P, T], I32, name="table_words")
+        nc.sync.dma_start(table_words[:], x_words[0].rearrange("p c r -> p (c r)").bitcast(I32))
+        n3_t = load_list("n3_t", n3)
+        n4_t = load_list("n4_t", n4)
+        nc.scalar.dma_start(table_scales[0:P:8, :].bitcast(I32), x_scales[0].bitcast(I32))
+        for i in range(4):
+            nc.scalar.dma_start(w_scales_raw[i:P:32, :].bitcast(I32), w1_scales[0, i:16:4, :].bitcast(I32))
+        w_words_raw = keep.tile([P, H], I32, name="w_words_raw")
+        nc.gpsimd.dma_start(w_words_raw[:], w1_words[0].rearrange("p c r -> p (c r)").bitcast(I32))
+        gain = keep.tile([P, PACK], F32, name="gain")
+        nc.gpsimd.dma_start(gain[:], gs.rearrange("(p t) o -> p (t o)", t=PACK))
+        warm = keep.tile([P, 1], F32, name="warm")
+        nc.vector.memset(warm[:], 0.0)
+        warm2 = keep.tile([P, 1], F32, name="warm2")
+        nc.scalar.activation(warm2[:], warm[:], ACT.Sigmoid)
+
+        def place_scale_rows(queue, plane, picked):
+            for i in range(4):
+                queue.dma_start(plane[i:P:32, :].bitcast(I32), picked[8 * i : P : 32, :].bitcast(I32))
+
+        def deal(name, src, dtype):
+            dealt = keep.tile([P, PACK * P], dtype, name=name, align_bytes=64)
+            nc.vector.tensor_copy(dealt[:].rearrange("p (t m) -> p t m", t=PACK), src.rearrange("p (m t) -> p t m", t=PACK))
+            return dealt
+
+        xq_picked = keep.tile([P, S], U8, name="xq_picked", align_bytes=64)
+        nc.vector.tensor_copy(xq_picked[:], table_scales[:].indirect(offs_t[:]))
+        place_scale_rows(nc.scalar, xq_scales, xq_picked)
+        w_scales = deal("w_scales", w_scales_raw[:], U8)
+        w_words = deal("w_words", w_words_raw[:].bitcast(U32), U32)
+        xq_words = keep.tile([P, S], U32, name="xq_words", align_bytes=64)
+        nc.vector.tensor_copy(xq_words[:], table_words[:].bitcast(U32).indirect(offs_t[:]))
+
+        y_rows = []
+        y_all = keep.tile([P, PACK, S], F32, name="y_all")
+        for t in range(PACK):
+            cols = slice(t * P, (t + 1) * P)
+            bank = psum.tile([P, S], F32, name="y_bank%d" % t)
+            nc.tensor.matmul_mx(out=bank[:], lhsT=w_words[:, cols].bitcast(FP8X4), lhsT_scale=w_scales[:, cols],
+                                rhs=xq_words[:].bitcast(FP8X4), rhs_scale=xq_scales[:], start=True, stop=True)
+            row = keep.tile([P, S], F32, name="y_row%d" % t)
+            nc.scalar.copy(row[:], bank[:])
+            nc.scalar.copy(y_all[:, t, :], bank[:])
+            y_rows.append(row)
+
+        cand_picked_words = keep.tile([P, C], U32, name="cand_picked_words", align_bytes=64)
+        nc.vector.tensor_copy(cand_picked_words[:], table_words[:].bitcast(U32).indirect(cand_t[:]))
+        cand_picked = keep.tile([P, C], U8, name="cand_picked", align_bytes=64)
+        nc.vector.tensor_copy(cand_picked[:], table_scales[:].indirect(cand_t[:]))
+        cand_words = deal("cand_words", cand_picked_words[:], U32)
+        cand_dealt = deal("cand_dealt", cand_picked[:], U8)
+        place_scale_rows(nc.sync, cand_scales, cand_dealt)
+
+        s_banks = [psum.tile([P, S], F32, name="s_bank%d" % t) for t in range(PACK)]
+        s_rows = [keep.tile([P, S], F32, name="s_row%d" % t) for t in range(PACK)]
+
+        s_all = keep.tile([P, PACK, S], F32, name="s_all")
+        for c, (start, width) in enumerate(Z_CHUNKS):
+            cols = slice(start, start + width)
+            pa = keep.tile([P, PACK, width], F32, name="pa%d" % c)
+            pb = keep.tile([P, PACK, width], F32, name="pb%d" % c)
+            hi = keep.tile([P, PACK, width], F32, name="hi%d" % c)
+            lo = keep.tile([P, PACK, width], F32, name="lo%d" % c)
+            z_bf = keep.tile([P, width, PACK], BF16, name="z_bf%d" % c, align_bytes=64)
+            for pair in range(2):
+                ts = slice(2 * pair, 2 * pair + 2)
+                for t in (2 * pair, 2 * pair + 1):
+                    nc.vector.tensor_tensor(pa[:, t, :], y_rows[t][:].indirect(entries(n1_t, start, width)), y_all[:, t, cols], ALU.subtract)
+                    nc.vector.tensor_tensor(pb[:, t, :], y_rows[t][:].indirect(entries(n2_t, start, width)), y_all[:, t, cols], ALU.subtract)
+                nc.vector.scalar_tensor_tensor(lo[:, ts, :], pa[:, ts, :], 0.0, pb[:, ts, :], ALU.min, ALU.min)
+                nc.vector.scalar_tensor_tensor(hi[:, ts, :], pa[:, ts, :], 0.0, pb[:, ts, :], ALU.max, ALU.max)
+                nc.vector.tensor_tensor(lo[:, ts, :], y_all[:, ts, cols], lo[:, ts, :], ALU.subtract)
+                nc.vector.scalar_tensor_tensor(pa[:, ts, :], lo[:, ts, :], 0.5, hi[:, ts, :], ALU.mult, ALU.add)
+                for t in (2 * pair, 2 * pair + 1):
+                    nc.scalar.activation(z_bf[:, :, t], pa[:, t, :], ACT.Copy, scale=gain[:, t : t + 1])
+            z_words = keep.tile([P, width], U32, name="z_words%d" % c, align_bytes=64)
+            z_scales = keep.tile([P, width], U8, name="z_scales%d" % c, align_bytes=64)
+            nc.vector.quantize_mx(out=z_words[:].bitcast(FP8X4), scales=z_scales[:], in_=z_bf[:].rearrange("p j t -> p (j t)"))
+            for t in range(PACK):
+                rows = slice(t * P, (t + 1) * P)
+                nc.tensor.matmul_mx(out=s_banks[t][:, cols], lhsT=cand_words[:, rows].bitcast(FP8X4), lhsT_scale=cand_scales[:, rows],
+                                    rhs=z_words[:].bitcast(FP8X4), rhs_scale=z_scales[:], start=True, stop=True)
+                nc.scalar.activation(s_rows[t][:, cols], s_banks[t][:, cols], ACT.Copy, scale=0.0625)
+            for t in range(PACK):
+                nc.scalar.activation(s_all[:, t, cols], s_banks[t][:, cols], ACT.Copy, scale=0.0625)
+
+        result = keep.tile([P, PACK, S], F32, name="result")
+        out_rows = out_0.rearrange("(p t) j -> p t j", t=PACK)
+        for t in range(PACK):
+            st = keep.tile([P, S], F32, name="st%d" % t)
+            for start, width in HALVES:
+                nc.vector.tensor_tensor(st[:, start : start + width], s_rows[t][:].indirect(entries(n3_t, start, width)), s_all[:, t, start : start + width], ALU.subtract)
+            gate = keep.tile([P, S], F32, name="gate%d" % t)
+            for start, width in HALVES:
+                nc.scalar.activation(gate[:, start : start + width], st[:].indirect(entries(n4_t, start, width)), ACT.Sigmoid)
+            if t < PACK - 1:
+                nc.vector.tensor_tensor(result[:, t, :], s_rows[t][:], gate[:], ALU.mult)
+                nc.sync.dma_start(out_rows[:, t, :], result[:, t, :])
+            else:
+                for start, width in HALVES:
+                    cols = slice(start, start + width)
+                    nc.vector.tensor_tensor(result[:, t, cols], s_rows[t][:, cols], gate[:, cols], ALU.mult)
+                    nc.sync.dma_start(out_rows[:, t, cols], result[:, t, cols])
+
+        out_scales = keep.tile([P, S], U8, name="out_scales", align_bytes=64)
+        words_hbm = out_1[0].rearrange("p c r -> p (c r)").bitcast(I32)
+        for h, (start, width) in enumerate(HALVES):
+            cols = slice(start, start + width)
+            o_bf = keep.tile([P, width, PACK], BF16, name="o_bf%d" % h, align_bytes=64)
+            if h == 0:
+                nc.scalar.copy(o_bf[:], result[:, :, cols].rearrange("p t j -> p j t"))
+            else:
+                nc.vector.tensor_copy(o_bf[:], result[:, :, cols].rearrange("p t j -> p j t"))
+            o_words = keep.tile([P, width], U32, name="o_words%d" % h, align_bytes=64)
+            nc.vector.quantize_mx(out=o_words[:].bitcast(FP8X4), scales=out_scales[:, cols], in_=o_bf[:].rearrange("p j t -> p (j t)"))
+            nc.sync.dma_start(words_hbm[:, cols], o_words[:].bitcast(I32))
+        for q in range(4):
+            queue = nc.sync if q % 2 == 0 else nc.scalar
+            queue.dma_start(out_2[0, 4 * q : 4 * q + 4, :].bitcast(I32), out_scales[32 * q : 32 * q + 4, :].bitcast(I32))

@@ -17,12 +17,12 @@ ACT = mybir.ActivationFunctionType
 
 P = 128
 PACK = 4
-Z_CHUNKS = ((0, 256), (256, 128), (384, 128))
-HALVES = ((0, 256), (256, 256))
+HALF = S // 2
+QUARTER = S // 4
 
 
-def entries(offsets, start, count):
-    return offsets[:, start // 16 : (start + count) // 16]
+def entries(offsets, cols):
+    return offsets[:, cols.start // 16 : cols.stop // 16]
 
 
 def tile_picked_hcandrangehopd_none_po_kernel(tc, x_words, x_scales, w1_words, w1_scales, gs, offs, n1, n2, cand, n3, n4, out_0, out_1, out_2):
@@ -48,6 +48,8 @@ def tile_picked_hcandrangehopd_none_po_kernel(tc, x_words, x_scales, w1_words, w
         cand_scales = zeroed_bytes("cand_scales", C)
         offs_t = load_list("offs_t", offs)
         cand_t = load_list("cand_t", cand)
+        w_words_raw = keep.tile([P, H], I32, name="w_words_raw", tag="undealt_words", align_bytes=64)
+        nc.sync.dma_start(w_words_raw[:], w1_words[0].rearrange("p c r -> p (c r)").bitcast(I32))
         n1_t = load_list("n1_t", n1)
         n2_t = load_list("n2_t", n2)
         table_words = keep.tile([P, T], I32, name="table_words")
@@ -57,8 +59,6 @@ def tile_picked_hcandrangehopd_none_po_kernel(tc, x_words, x_scales, w1_words, w
         nc.scalar.dma_start(table_scales[0:P:8, :].bitcast(I32), x_scales[0].bitcast(I32))
         for i in range(4):
             nc.scalar.dma_start(w_scales_raw[i:P:32, :].bitcast(I32), w1_scales[0, i:16:4, :].bitcast(I32))
-        w_words_raw = keep.tile([P, H], I32, name="w_words_raw")
-        nc.gpsimd.dma_start(w_words_raw[:], w1_words[0].rearrange("p c r -> p (c r)").bitcast(I32))
         gain = keep.tile([P, PACK], F32, name="gain")
         nc.gpsimd.dma_start(gain[:], gs.rearrange("(p t) o -> p (t o)", t=PACK))
         warm = keep.tile([P, 1], F32, name="warm")
@@ -66,106 +66,129 @@ def tile_picked_hcandrangehopd_none_po_kernel(tc, x_words, x_scales, w1_words, w
         warm2 = keep.tile([P, 1], F32, name="warm2")
         nc.scalar.activation(warm2[:], warm[:], ACT.Sigmoid)
 
-        def place_scale_rows(queue, plane, picked):
+        def place_scale_rows(plane, picked):
             for i in range(4):
-                queue.dma_start(plane[i:P:32, :].bitcast(I32), picked[8 * i : P : 32, :].bitcast(I32))
+                nc.sync.dma_start(plane[i:P:32, :].bitcast(I32), picked[8 * i : P : 32, :].bitcast(I32))
 
-        def deal(name, src, dtype):
+        def deal(name, src, dtype, run):
             dealt = keep.tile([P, PACK * P], dtype, name=name, align_bytes=64)
-            nc.vector.tensor_copy(dealt[:].rearrange("p (t m) -> p t m", t=PACK), src.rearrange("p (m t) -> p t m", t=PACK))
+            nc.vector.tensor_copy(dealt[:].rearrange("p (t c i) -> p c t i", t=PACK, i=run), src.rearrange("p (c i t) -> p c t i", t=PACK, i=run))
             return dealt
 
         xq_picked = keep.tile([P, S], U8, name="xq_picked", align_bytes=64)
         nc.vector.tensor_copy(xq_picked[:], table_scales[:].indirect(offs_t[:]))
-        place_scale_rows(nc.scalar, xq_scales, xq_picked)
-        w_scales = deal("w_scales", w_scales_raw[:], U8)
-        w_words = deal("w_words", w_words_raw[:].bitcast(U32), U32)
+        place_scale_rows(xq_scales, xq_picked)
         xq_words = keep.tile([P, S], U32, name="xq_words", align_bytes=64)
         nc.vector.tensor_copy(xq_words[:], table_words[:].bitcast(U32).indirect(offs_t[:]))
+        w_words = deal("w_words", w_words_raw[:].bitcast(U32), U32, 4)
+        w_scales = deal("w_scales", w_scales_raw[:], U8, 16)
 
-        y_rows = []
-        y_all = keep.tile([P, PACK, S], F32, name="y_all")
+        first, second = slice(0, S), slice(S, 2 * S)
+        y_rows = [keep.tile([P, S], F32, name="y_row%d" % t) for t in range(PACK)]
+        s_and_y = [keep.tile([P, 2 * S], F32, name="s_and_y%d" % t) for t in range(PACK)]
+        st_and_s = [keep.tile([P, 2 * S], F32, name="st_and_s%d" % t) for t in range(PACK)]
+        y_plain = [pair[:, second] for pair in s_and_y]
+        s_plain = [pair[:, second] for pair in st_and_s]
         for t in range(PACK):
             cols = slice(t * P, (t + 1) * P)
             bank = psum.tile([P, S], F32, name="y_bank%d" % t)
             nc.tensor.matmul_mx(out=bank[:], lhsT=w_words[:, cols].bitcast(FP8X4), lhsT_scale=w_scales[:, cols],
                                 rhs=xq_words[:].bitcast(FP8X4), rhs_scale=xq_scales[:], start=True, stop=True)
-            row = keep.tile([P, S], F32, name="y_row%d" % t)
-            nc.scalar.copy(row[:], bank[:])
-            nc.scalar.copy(y_all[:, t, :], bank[:])
-            y_rows.append(row)
+            nc.scalar.copy(y_rows[t][:], bank[:])
+            nc.scalar.copy(y_plain[t], bank[:])
 
-        cand_picked_words = keep.tile([P, C], U32, name="cand_picked_words", align_bytes=64)
-        nc.vector.tensor_copy(cand_picked_words[:], table_words[:].bitcast(U32).indirect(cand_t[:]))
         cand_picked = keep.tile([P, C], U8, name="cand_picked", align_bytes=64)
         nc.vector.tensor_copy(cand_picked[:], table_scales[:].indirect(cand_t[:]))
-        cand_words = deal("cand_words", cand_picked_words[:], U32)
-        cand_dealt = deal("cand_dealt", cand_picked[:], U8)
-        place_scale_rows(nc.sync, cand_scales, cand_dealt)
+        cand_picked_words = keep.tile([P, C], U32, name="cand_picked_words", tag="undealt_words", align_bytes=64)
+        nc.vector.tensor_copy(cand_picked_words[:], table_words[:].bitcast(U32).indirect(cand_t[:]))
+        cand_dealt = deal("cand_dealt", cand_picked[:], U8, 16)
+        cand_words = deal("cand_words", cand_picked_words[:], U32, 4)
+        place_scale_rows(cand_scales, cand_dealt)
 
         s_banks = [psum.tile([P, S], F32, name="s_bank%d" % t) for t in range(PACK)]
-        s_rows = [keep.tile([P, S], F32, name="s_row%d" % t) for t in range(PACK)]
+        da = keep.tile([P, PACK, S], F32, name="da")
+        db = keep.tile([P, PACK, S], F32, name="db")
+        hi = keep.tile([P, PACK, S], F32, name="hi")
+        lo = keep.tile([P, PACK, S], F32, name="lo")
+        z_raw = keep.tile([P, PACK, S], F32, name="z_raw")
+        z_bf = [keep.tile([P, HALF, PACK], BF16, name="z_bf%d" % h, align_bytes=64) for h in range(2)]
 
-        s_all = keep.tile([P, PACK, S], F32, name="s_all")
-        for c, (start, width) in enumerate(Z_CHUNKS):
-            cols = slice(start, start + width)
-            pa = keep.tile([P, PACK, width], F32, name="pa%d" % c)
-            pb = keep.tile([P, PACK, width], F32, name="pb%d" % c)
-            hi = keep.tile([P, PACK, width], F32, name="hi%d" % c)
-            lo = keep.tile([P, PACK, width], F32, name="lo%d" % c)
-            z_bf = keep.tile([P, width, PACK], BF16, name="z_bf%d" % c, align_bytes=64)
-            for pair in range(2):
-                ts = slice(2 * pair, 2 * pair + 2)
-                for t in (2 * pair, 2 * pair + 1):
-                    nc.vector.tensor_tensor(pa[:, t, :], y_rows[t][:].indirect(entries(n1_t, start, width)), y_all[:, t, cols], ALU.subtract)
-                    nc.vector.tensor_tensor(pb[:, t, :], y_rows[t][:].indirect(entries(n2_t, start, width)), y_all[:, t, cols], ALU.subtract)
-                nc.vector.scalar_tensor_tensor(lo[:, ts, :], pa[:, ts, :], 0.0, pb[:, ts, :], ALU.min, ALU.min)
-                nc.vector.scalar_tensor_tensor(hi[:, ts, :], pa[:, ts, :], 0.0, pb[:, ts, :], ALU.max, ALU.max)
-                nc.vector.tensor_tensor(lo[:, ts, :], y_all[:, ts, cols], lo[:, ts, :], ALU.subtract)
-                nc.vector.scalar_tensor_tensor(pa[:, ts, :], lo[:, ts, :], 0.5, hi[:, ts, :], ALU.mult, ALU.add)
-                for t in (2 * pair, 2 * pair + 1):
-                    nc.scalar.activation(z_bf[:, :, t], pa[:, t, :], ACT.Copy, scale=gain[:, t : t + 1])
-            z_words = keep.tile([P, width], U32, name="z_words%d" % c, align_bytes=64)
-            z_scales = keep.tile([P, width], U8, name="z_scales%d" % c, align_bytes=64)
-            nc.vector.quantize_mx(out=z_words[:].bitcast(FP8X4), scales=z_scales[:], in_=z_bf[:].rearrange("p j t -> p (j t)"))
+        def difference(out, offsets, t, cols):
+            nc.vector.tensor_tensor(out[:, t, cols], y_rows[t][:].indirect(entries(offsets, cols)), y_plain[t][:, cols], ALU.subtract)
+
+        def scores(cols):
+            width = cols.stop - cols.start
+            half, at = divmod(cols.start, HALF)
+            z_words = keep.tile([P, width], U32, name="z_words%d" % cols.start, align_bytes=64)
+            z_scales = keep.tile([P, width], U8, name="z_scales%d" % cols.start, align_bytes=64)
+            nc.vector.quantize_mx(out=z_words[:].bitcast(FP8X4), scales=z_scales[:],
+                                  in_=z_bf[half][:, at : at + width, :].rearrange("p j t -> p (j t)"))
             for t in range(PACK):
                 rows = slice(t * P, (t + 1) * P)
                 nc.tensor.matmul_mx(out=s_banks[t][:, cols], lhsT=cand_words[:, rows].bitcast(FP8X4), lhsT_scale=cand_scales[:, rows],
                                     rhs=z_words[:].bitcast(FP8X4), rhs_scale=z_scales[:], start=True, stop=True)
-                nc.scalar.activation(s_rows[t][:, cols], s_banks[t][:, cols], ACT.Copy, scale=0.0625)
-            for t in range(PACK):
-                nc.scalar.activation(s_all[:, t, cols], s_banks[t][:, cols], ACT.Copy, scale=0.0625)
+                nc.scalar.activation(s_and_y[t][:, cols], s_banks[t][:, cols], ACT.Copy, scale=0.0625)
+                nc.scalar.activation(s_plain[t][:, cols], s_banks[t][:, cols], ACT.Copy, scale=0.0625)
+
+        pieces = [(t, slice(0, HALF)) for t in range(PACK)]
+        pieces = pieces + [(t, slice(HALF, S)) for t in range(PACK - 1)]
+        pieces = pieces + [(PACK - 1, slice(HALF, HALF + QUARTER)), (PACK - 1, slice(HALF + QUARTER, S))]
+        difference(da, n1_t, *pieces[0])
+        difference(db, n2_t, *pieces[0])
+        for k, (t, cols) in enumerate(pieces):
+            ahead = pieces[k + 1 : k + 2]
+            nc.vector.scalar_tensor_tensor(lo[:, t, cols], da[:, t, cols], 0.0, db[:, t, cols], ALU.min, ALU.min)
+            nc.vector.scalar_tensor_tensor(hi[:, t, cols], da[:, t, cols], 0.0, db[:, t, cols], ALU.max, ALU.max)
+            for piece in ahead:
+                difference(da, n1_t, *piece)
+            nc.vector.tensor_tensor(lo[:, t, cols], y_plain[t][:, cols], lo[:, t, cols], ALU.subtract)
+            for piece in ahead:
+                difference(db, n2_t, *piece)
+            if k == len(pieces) - 1:
+                scores(pieces[k - 1][1])
+            nc.vector.scalar_tensor_tensor(z_raw[:, t, cols], lo[:, t, cols], 0.5, hi[:, t, cols], ALU.mult, ALU.add)
+            half, at = divmod(cols.start, HALF)
+            nc.scalar.activation(z_bf[half][:, at : at + cols.stop - cols.start, t], z_raw[:, t, cols], ACT.Copy, scale=gain[:, t : t + 1])
+            if k == PACK:
+                scores(slice(0, HALF))
+        scores(pieces[-1][1])
 
         result = keep.tile([P, PACK, S], F32, name="result")
+        gate = keep.tile([P, PACK, S], F32, name="gate")
         out_rows = out_0.rearrange("(p t) j -> p t j", t=PACK)
+        halves = (slice(0, HALF), slice(HALF, S))
         for t in range(PACK):
-            st = keep.tile([P, S], F32, name="st%d" % t)
-            for start, width in HALVES:
-                nc.vector.tensor_tensor(st[:, start : start + width], s_rows[t][:].indirect(entries(n3_t, start, width)), s_all[:, t, start : start + width], ALU.subtract)
-            gate = keep.tile([P, S], F32, name="gate%d" % t)
-            for start, width in HALVES:
-                nc.scalar.activation(gate[:, start : start + width], st[:].indirect(entries(n4_t, start, width)), ACT.Sigmoid)
-            if t < PACK - 1:
-                nc.vector.tensor_tensor(result[:, t, :], s_rows[t][:], gate[:], ALU.mult)
-                nc.sync.dma_start(out_rows[:, t, :], result[:, t, :])
-            else:
-                for start, width in HALVES:
-                    cols = slice(start, start + width)
-                    nc.vector.tensor_tensor(result[:, t, cols], s_rows[t][:, cols], gate[:, cols], ALU.mult)
-                    nc.sync.dma_start(out_rows[:, t, cols], result[:, t, cols])
+            nc.vector.tensor_tensor(st_and_s[t][:, first], s_and_y[t][:].indirect(n3_t[:]), s_plain[t], ALU.subtract)
+            for cols in halves if t == PACK - 1 else (first,):
+                nc.scalar.activation(gate[:, t, cols], st_and_s[t][:].indirect(entries(n4_t, cols)), ACT.Sigmoid)
+
+        def finish(t, cols):
+            nc.vector.tensor_tensor(result[:, t, cols], s_plain[t][:, cols], gate[:, t, cols], ALU.mult)
+            nc.sync.dma_start(out_rows[:, t, cols], result[:, t, cols])
+
+        finish(0, first)
+        finish(1, first)
+        for cols in halves:
+            finish(2, cols)
+            finish(3, cols)
 
         out_scales = keep.tile([P, S], U8, name="out_scales", align_bytes=64)
         words_hbm = out_1[0].rearrange("p c r -> p (c r)").bitcast(I32)
-        for h, (start, width) in enumerate(HALVES):
-            cols = slice(start, start + width)
-            o_bf = keep.tile([P, width, PACK], BF16, name="o_bf%d" % h, align_bytes=64)
+        rounded = []
+        for h, cols in enumerate(halves):
+            o_bf = keep.tile([P, HALF, PACK], BF16, name="o_bf%d" % h, align_bytes=64)
+            dst = o_bf[:].rearrange("p (c i) t -> p c t i", i=4)
+            src = result[:, :, cols].rearrange("p t (c i) -> p c t i", i=4)
             if h == 0:
-                nc.scalar.copy(o_bf[:], result[:, :, cols].rearrange("p t j -> p j t"))
+                nc.scalar.copy(dst, src)
             else:
-                nc.vector.tensor_copy(o_bf[:], result[:, :, cols].rearrange("p t j -> p j t"))
-            o_words = keep.tile([P, width], U32, name="o_words%d" % h, align_bytes=64)
-            nc.vector.quantize_mx(out=o_words[:].bitcast(FP8X4), scales=out_scales[:, cols], in_=o_bf[:].rearrange("p j t -> p (j t)"))
+                nc.vector.tensor_copy(dst, src)
+            rounded.append(o_bf)
+        for h in (1, 0):
+            cols = halves[h]
+            o_words = keep.tile([P, HALF], U32, name="o_words%d" % h, align_bytes=64)
+            nc.vector.quantize_mx(out=o_words[:].bitcast(FP8X4), scales=out_scales[:, cols], in_=rounded[h][:].rearrange("p j t -> p (j t)"))
             nc.sync.dma_start(words_hbm[:, cols], o_words[:].bitcast(I32))
         for q in range(4):
-            queue = nc.sync if q % 2 == 0 else nc.scalar
+            queue = nc.scalar if q % 2 == 0 else nc.sync
             queue.dma_start(out_2[0, 4 * q : 4 * q + 4, :].bitcast(I32), out_scales[32 * q : 32 * q + 4, :].bitcast(I32))

from contextlib import ExitStack

import concourse.mybir as mybir

K, T, S, H, C = 512, 2048, 512, 512, 512
FLOPS = 2 * K * H * S + 2 * K * C * S

F32 = mybir.dt.float32
BF16 = mybir.dt.bfloat16
I32 = mybir.dt.int32
U32 = mybir.dt.uint32
U16 = mybir.dt.uint16
U8 = mybir.dt.uint8
FP8X4 = mybir.dt.float8_e4m3fn_x4
ALU = mybir.AluOpType
ACT = mybir.ActivationFunctionType

P = 128
PACK = 4
HALF = S // 2
QUARTER = S // 4


def entries(offsets, cols):
    return offsets[:, cols.start // 16 : cols.stop // 16]


def tile_picked_hcandrangehopd_none_po_kernel(tc, x_words, x_scales, w1_words, w1_scales, gs, offs, n1, n2, cand, n3, n4, out_0, out_1, out_2):
    nc = tc.nc
    with ExitStack() as ctx:
        lists = ctx.enter_context(tc.tile_pool(name="lists", bufs=1))
        keep = ctx.enter_context(tc.tile_pool(name="keep", bufs=1))
        psum = ctx.enter_context(tc.psum_pool(name="psum", bufs=1))

        def load_list(name, src):
            held = lists.tile([P, S // 16], U16, name=name)
            nc.sync.dma_start(held[:], src)
            return held

        def zeroed_bytes(name, width):
            held = keep.tile([P, width], U8, name=name, align_bytes=64)
            nc.vector.memset(held[:].bitcast(I32), 0)
            return held

        table_scales = zeroed_bytes("table_scales", T)
        w_scales_raw = zeroed_bytes("w_scales_raw", H)
        xq_scales = zeroed_bytes("xq_scales", S)
        cand_scales = zeroed_bytes("cand_scales", C)
        offs_t = load_list("offs_t", offs)
        cand_t = load_list("cand_t", cand)
        w_words_raw = keep.tile([P, H], I32, name="w_words_raw", tag="undealt_words", align_bytes=64)
        nc.sync.dma_start(w_words_raw[:], w1_words[0].rearrange("p c r -> p (c r)").bitcast(I32))
        n1_t = load_list("n1_t", n1)
        n2_t = load_list("n2_t", n2)
        table_words = keep.tile([P, T], I32, name="table_words")
        nc.sync.dma_start(table_words[:], x_words[0].rearrange("p c r -> p (c r)").bitcast(I32))
        n3_t = load_list("n3_t", n3)
        n4_t = load_list("n4_t", n4)
        nc.scalar.dma_start(table_scales[0:P:8, :].bitcast(I32), x_scales[0].bitcast(I32))
        for i in range(4):
            nc.scalar.dma_start(w_scales_raw[i:P:32, :].bitcast(I32), w1_scales[0, i:16:4, :].bitcast(I32))
        gain = keep.tile([P, PACK], F32, name="gain")
        nc.gpsimd.dma_start(gain[:], gs.rearrange("(p t) o -> p (t o)", t=PACK))
        warm = keep.tile([P, 1], F32, name="warm")
        nc.vector.memset(warm[:], 0.0)
        warm2 = keep.tile([P, 1], F32, name="warm2")
        nc.scalar.activation(warm2[:], warm[:], ACT.Sigmoid)

        def place_scale_rows(plane, picked):
            for i in range(4):
                nc.sync.dma_start(plane[i:P:32, :].bitcast(I32), picked[8 * i : P : 32, :].bitcast(I32))

        def deal(name, src, dtype, run):
            dealt = keep.tile([P, PACK * P], dtype, name=name, align_bytes=64)
            nc.vector.tensor_copy(dealt[:].rearrange("p (t c i) -> p c t i", t=PACK, i=run), src.rearrange("p (c i t) -> p c t i", t=PACK, i=run))
            return dealt

        xq_picked = keep.tile([P, S], U8, name="xq_picked", align_bytes=64)
        nc.vector.tensor_copy(xq_picked[:], table_scales[:].indirect(offs_t[:]))
        place_scale_rows(xq_scales, xq_picked)
        xq_words = keep.tile([P, S], U32, name="xq_words", align_bytes=64)
        nc.vector.tensor_copy(xq_words[:], table_words[:].bitcast(U32).indirect(offs_t[:]))
        w_words = deal("w_words", w_words_raw[:].bitcast(U32), U32, 4)
        w_scales = deal("w_scales", w_scales_raw[:], U8, 16)

        first, second = slice(0, S), slice(S, 2 * S)
        y_rows = [keep.tile([P, S], F32, name="y_row%d" % t) for t in range(PACK)]
        s_and_y = [keep.tile([P, 2 * S], F32, name="s_and_y%d" % t) for t in range(PACK)]
        st_and_s = [keep.tile([P, 2 * S], F32, name="st_and_s%d" % t) for t in range(PACK)]
        y_plain = [pair[:, second] for pair in s_and_y]
        s_plain = [pair[:, second] for pair in st_and_s]
        for t in range(PACK):
            cols = slice(t * P, (t + 1) * P)
            bank = psum.tile([P, S], F32, name="y_bank%d" % t)
            nc.tensor.matmul_mx(out=bank[:], lhsT=w_words[:, cols].bitcast(FP8X4), lhsT_scale=w_scales[:, cols],
                                rhs=xq_words[:].bitcast(FP8X4), rhs_scale=xq_scales[:], start=True, stop=True)
            nc.scalar.copy(y_rows[t][:], bank[:])
            nc.scalar.copy(y_plain[t], bank[:])

        cand_picked = keep.tile([P, C], U8, name="cand_picked", align_bytes=64)
        nc.vector.tensor_copy(cand_picked[:], table_scales[:].indirect(cand_t[:]))
        cand_picked_words = keep.tile([P, C], U32, name="cand_picked_words", tag="undealt_words", align_bytes=64)
        nc.vector.tensor_copy(cand_picked_words[:], table_words[:].bitcast(U32).indirect(cand_t[:]))
        cand_dealt = deal("cand_dealt", cand_picked[:], U8, 16)
        cand_words = deal("cand_words", cand_picked_words[:], U32, 4)
        place_scale_rows(cand_scales, cand_dealt)

        s_banks = [psum.tile([P, S], F32, name="s_bank%d" % t) for t in range(PACK)]
        da = keep.tile([P, PACK, S], F32, name="da")
        db = keep.tile([P, PACK, S], F32, name="db")
        hi = keep.tile([P, PACK, S], F32, name="hi")
        lo = keep.tile([P, PACK, S], F32, name="lo")
        z_raw = keep.tile([P, PACK, S], F32, name="z_raw")
        z_bf = [keep.tile([P, HALF, PACK], BF16, name="z_bf%d" % h, align_bytes=64) for h in range(2)]

        def difference(out, offsets, t, cols):
            nc.vector.tensor_tensor(out[:, t, cols], y_rows[t][:].indirect(entries(offsets, cols)), y_plain[t][:, cols], ALU.subtract)

        def scores(cols):
            width = cols.stop - cols.start
            half, at = divmod(cols.start, HALF)
            z_words = keep.tile([P, width], U32, name="z_words%d" % cols.start, align_bytes=64)
            z_scales = keep.tile([P, width], U8, name="z_scales%d" % cols.start, align_bytes=64)
            nc.vector.quantize_mx(out=z_words[:].bitcast(FP8X4), scales=z_scales[:],
                                  in_=z_bf[half][:, at : at + width, :].rearrange("p j t -> p (j t)"))
            for t in range(PACK):
                rows = slice(t * P, (t + 1) * P)
                nc.tensor.matmul_mx(out=s_banks[t][:, cols], lhsT=cand_words[:, rows].bitcast(FP8X4), lhsT_scale=cand_scales[:, rows],
                                    rhs=z_words[:].bitcast(FP8X4), rhs_scale=z_scales[:], start=True, stop=True)
                nc.scalar.activation(s_and_y[t][:, cols], s_banks[t][:, cols], ACT.Copy, scale=0.0625)
                nc.scalar.activation(s_plain[t][:, cols], s_banks[t][:, cols], ACT.Copy, scale=0.0625)

        pieces = [(t, slice(0, HALF)) for t in range(PACK)]
        pieces = pieces + [(t, slice(HALF, S)) for t in range(PACK - 1)]
        pieces = pieces + [(PACK - 1, slice(HALF, HALF + QUARTER)), (PACK - 1, slice(HALF + QUARTER, S))]
        difference(da, n1_t, *pieces[0])
        difference(db, n2_t, *pieces[0])
        for k, (t, cols) in enumerate(pieces):
            ahead = pieces[k + 1 : k + 2]
            nc.vector.scalar_tensor_tensor(lo[:, t, cols], da[:, t, cols], 0.0, db[:, t, cols], ALU.min, ALU.min)
            nc.vector.scalar_tensor_tensor(hi[:, t, cols], da[:, t, cols], 0.0, db[:, t, cols], ALU.max, ALU.max)
            for piece in ahead:
                difference(da, n1_t, *piece)
            nc.vector.tensor_tensor(lo[:, t, cols], y_plain[t][:, cols], lo[:, t, cols], ALU.subtract)
            for piece in ahead:
                difference(db, n2_t, *piece)
            if k == len(pieces) - 1:
                scores(pieces[k - 1][1])
            nc.vector.scalar_tensor_tensor(z_raw[:, t, cols], lo[:, t, cols], 0.5, hi[:, t, cols], ALU.mult, ALU.add)
            half, at = divmod(cols.start, HALF)
            nc.scalar.activation(z_bf[half][:, at : at + cols.stop - cols.start, t], z_raw[:, t, cols], ACT.Copy, scale=gain[:, t : t + 1])
            if k == PACK:
                scores(slice(0, HALF))
        scores(pieces[-1][1])

        result = keep.tile([P, PACK, S], F32, name="result")
        gate = keep.tile([P, PACK, S], F32, name="gate")
        out_rows = out_0.rearrange("(p t) j -> p t j", t=PACK)
        halves = (slice(0, HALF), slice(HALF, S))
        for t in range(PACK):
            nc.vector.tensor_tensor(st_and_s[t][:, first], s_and_y[t][:].indirect(n3_t[:]), s_plain[t], ALU.subtract)
            for cols in halves if t == PACK - 1 else (first,):
                nc.scalar.activation(gate[:, t, cols], st_and_s[t][:].indirect(entries(n4_t, cols)), ACT.Sigmoid)

        def finish(t, cols):
            nc.vector.tensor_tensor(result[:, t, cols], s_plain[t][:, cols], gate[:, t, cols], ALU.mult)
            nc.sync.dma_start(out_rows[:, t, cols], result[:, t, cols])

        finish(0, first)
        finish(1, first)
        for cols in halves:
            finish(2, cols)
            finish(3, cols)

        out_scales = keep.tile([P, S], U8, name="out_scales", align_bytes=64)
        words_hbm = out_1[0].rearrange("p c r -> p (c r)").bitcast(I32)
        rounded = []
        for h, cols in enumerate(halves):
            o_bf = keep.tile([P, HALF, PACK], BF16, name="o_bf%d" % h, align_bytes=64)
            dst = o_bf[:].rearrange("p (c i) t -> p c t i", i=4)
            src = result[:, :, cols].rearrange("p t (c i) -> p c t i", i=4)
            if h == 0:
                nc.scalar.copy(dst, src)
            else:
                nc.vector.tensor_copy(dst, src)
            rounded.append(o_bf)
        for h in (1, 0):
            cols = halves[h]
            o_words = keep.tile([P, HALF], U32, name="o_words%d" % h, align_bytes=64)
            nc.vector.quantize_mx(out=o_words[:].bitcast(FP8X4), scales=out_scales[:, cols], in_=rounded[h][:].rearrange("p j t -> p (j t)"))
            nc.sync.dma_start(words_hbm[:, cols], o_words[:].bitcast(I32))
        for q in range(4):
            queue = nc.scalar if q % 2 == 0 else nc.sync
            queue.dma_start(out_2[0, 4 * q : 4 * q + 4, :].bitcast(I32), out_scales[32 * q : 32 * q + 4, :].bitcast(I32))
